import numpy as np
import ml_dtypes


def mxq(x, axis, fmt="e4m3"):
    dtype, down = {"e4m3": (ml_dtypes.float8_e4m3fn, 7), "e5m2": (ml_dtypes.float8_e5m2, 14)}[fmt]
    v = np.moveaxis(np.asarray(x, np.float32).astype(ml_dtypes.bfloat16).astype(np.float64), axis, -1)
    blocks = v.reshape(v.shape[:-1] + (-1, 32))
    amax = np.abs(blocks).max(-1, keepdims=True)
    byte = np.maximum(np.where(amax > 0, np.frexp(amax)[1] - 1 + 127, 0) - down, 1)
    scale = np.exp2(byte - 127.0)
    codes = (blocks / scale).astype(np.float32).astype(dtype).astype(np.float64)
    return np.moveaxis((codes * scale).reshape(v.shape), -1, axis)


WIDE = False


def mx_kscale(k):
    if not WIDE:
        return np.ones(k)
    levels = np.array([10, -10, 5, -5, 0])
    if k % 512:
        return np.exp2(np.random.permutation(np.resize(levels, k // 32))).repeat(32)
    a = np.empty((k // 512, 16))
    for p in range(k // 512):
        a[p, :8] = np.random.permutation(np.resize(levels, 8))
        for g in range(8):
            far = levels[np.abs(levels - a[p, g]) >= 10]
            a[p, g + 8] = far[np.random.randint(len(far))]
    return np.exp2(a.ravel()).repeat(32)


BF16 = ml_dtypes.bfloat16


def bf(x):
    return np.asarray(x, np.float32).astype(BF16)


def f64(x):
    return np.asarray(x).astype(np.float64)


E2M1 = np.array([0.0, 0.5, 1.0, 1.5, 2.0, 3.0, 4.0, 6.0, -0.0, -0.5, -1.0, -1.5, -2.0, -3.0, -4.0, -6.0])


def pack_weight(w, fmt):
    k, n = w.shape
    w = f64(bf(w)).reshape(k // 32, 32, n)
    amax = np.abs(w).max(1)
    if fmt == "e4m3":
        byte = np.frexp(amax)[1] - 1 + 127 - 7
    else:
        mant, ex = np.frexp(amax / 6.0)
        byte = np.where(mant > 0.5, ex, ex - 1) + 127
    byte = np.clip(np.where(amax > 0, byte, 1), 1, 254)
    scaled = (w * np.exp2(127.0 - byte)[:, None, :]).reshape(k, n).astype(np.float32)
    by_word = np.ascontiguousarray(scaled.reshape(k // 512, 128, 4, n).transpose(0, 1, 3, 2))
    if fmt == "e4m3":
        words = by_word.astype(ml_dtypes.float8_e4m3fn).view(np.uint8)
    else:
        c = by_word.astype(ml_dtypes.float4_e2m1fn).view(np.uint8) & 0xF
        words = c[..., 0::2] | (c[..., 1::2] << 4)
    return np.ascontiguousarray(words), np.ascontiguousarray(byte.astype(np.uint8).reshape(k // 512, 16, n))


def unpack_weight(words, scales, fmt):
    g, p, n, _ = words.shape
    if fmt == "e4m3":
        vals = np.ascontiguousarray(words).view(ml_dtypes.float8_e4m3fn).astype(np.float64)
    else:
        nib = np.empty((g, p, n, 4), np.uint8)
        nib[..., 0::2] = words & 0xF
        nib[..., 1::2] = words >> 4
        vals = E2M1[nib]
    vals = vals * np.repeat(np.exp2(scales.astype(np.float64) - 127.0), 8, axis=1)[..., None]
    return vals.transpose(0, 1, 3, 2).reshape(g * 512, n)
def pack4(w):
    words, scales = pack_weight(w, "e2m1")
    return words.reshape(words.shape[0], 128, -1), scales


def unpack4(words, scales):
    return unpack_weight(words.reshape(words.shape[0], 128, -1, 2), scales, "e2m1")


def planes(Y):
    n, m = Y.shape
    b = f64(bf(Y)).reshape(n // 32, 32, m)
    amax = np.abs(b).max(1)
    byte = np.clip(np.where(amax > 0, np.frexp(amax)[1] - 1 + 127 - 7, 1), 1, 254)
    codes = (b * np.exp2(127.0 - byte)[:, None, :]).reshape(n, m).astype(np.float32).astype(ml_dtypes.float8_e4m3fn).view(np.uint8)
    words = codes.reshape(n // 512, 128, 4, m).transpose(0, 1, 3, 2)
    return np.ascontiguousarray(words), np.ascontiguousarray(byte.astype(np.uint8).reshape(n // 512, 16, m))


B, Q, D, C = 16, 128, 1536, 1024


def setup_inputs():
    s = mx_kscale(D)
    x = np.random.randn(B * Q, D) * s
    x_words, x_scales = pack_weight(x.T, "e4m3")
    w = np.random.randn(D, C) / np.sqrt(D) / s[:, None]
    bias = 0.4 * np.random.randn(C)
    spread = np.exp(0.8 * np.random.randn(C))
    gain = spread * (1.0 + 0.1 * np.random.rand(C))
    query_embed = 0.5 * spread * np.random.randn(Q, C)
    return {
        "x_words": x_words,
        "x_scales": x_scales,
        "w": bf(w),
        "bias": bf(bias),
        "gain": bf(gain),
        "query_embed": bf(query_embed),
    }


def reference(x_words, x_scales, w, bias, gain, query_embed):
    x = unpack_weight(x_words, x_scales, "e4m3")
    wq = mxq(f64(w), 0, "e4m3")
    z = x.T @ wq
    h = np.maximum(z + f64(bias), 0.0) * f64(gain)
    y = h.reshape(B, Q, C) + f64(query_embed)
    Y = y.reshape(B * Q, C).T
    words, scales = planes(Y)
    return y, words, scales

@@ -1,0 +1,238 @@
+from contextlib import ExitStack
+
+import concourse.mybir as mybir
+from concourse.masks import make_identity
+
+B, Q, D, C = 16, 128, 1536, 1024
+TOKENS = B * Q
+FLOPS = 2 * TOKENS * D * C
+
+F32 = mybir.dt.float32
+BF16 = mybir.dt.bfloat16
+I32 = mybir.dt.int32
+U32 = mybir.dt.uint32
+U8 = mybir.dt.uint8
+FP8X4 = mybir.dt.float8_e4m3fn_x4
+ALU = mybir.AluOpType
+ACT = mybir.ActivationFunctionType
+
+P = 128
+PACK = 4
+GROUP = P * PACK
+K_GROUPS = D // GROUP
+C_GROUPS = C // GROUP
+TOK_TILE = 512
+TOK_TILES = TOKENS // TOK_TILE
+IMAGES = TOK_TILE // Q
+WORK_BANKS = 7
+UNIT_WIDTHS = ((512, 512, 512, 512), (512, 512, 512, 256, 256))
+BEFORE_TURN = 3
+
+
+def tile_mask_query_embed_planes_g6_kernel(tc, x_words, x_scales, w, bias, gain, query_embed, out_0, out_1, out_2):
+    nc = tc.nc
+    units = []
+    for cg, widths in enumerate(UNIT_WIDTHS):
+        start = 0
+        for width in widths:
+            units.append((cg, start, width))
+            start += width
+    last = len(units) - 1
+
+    with ExitStack() as ctx:
+        keep = ctx.enter_context(tc.tile_pool(name="keep", bufs=1))
+        work = ctx.enter_context(tc.tile_pool(name="work", bufs=2))
+        psum = ctx.enter_context(tc.psum_pool(name="psum", bufs=1))
+        ctx.enter_context(tc.manual_schedule())
+
+        x_codes = keep.tile([P, K_GROUPS, TOKENS], U32, align_bytes=64)
+        x_plane = keep.tile([P, TOKENS], U8, align_bytes=64)
+        w_raw = keep.tile([P, C_GROUPS, K_GROUPS, PACK, GROUP], BF16, align_bytes=64)
+        w_grouped = keep.tile([P, C_GROUPS, K_GROUPS, PACK, P, PACK], BF16, align_bytes=64)
+        w_codes = keep.tile([P, C_GROUPS, K_GROUPS, GROUP], U32, align_bytes=64)
+        w_plane = keep.tile([P, C_GROUPS, K_GROUPS, GROUP], U8, align_bytes=64)
+        y_codes = keep.tile([P, C_GROUPS, TOKENS], U32, align_bytes=64)
+        y_plane = keep.tile([P, C_GROUPS, TOKENS], U8, align_bytes=64)
+        embed = keep.tile([P, C], BF16)
+        bias_raw = keep.tile([P, C_GROUPS, PACK], BF16)
+        gain_raw = keep.tile([P, C_GROUPS, PACK], BF16)
+        bias_col = keep.tile([P, C_GROUPS, PACK], F32)
+        gain_col = keep.tile([P, C_GROUPS, PACK], F32)
+        ident_bf16 = keep.tile([P, P], BF16)
+        ident_f32 = keep.tile([P, P], F32)
+        warm_in = keep.tile([P, 1], F32)
+        warm_out = keep.tile([P, 1], F32)
+        embed_t = psum.tile([P, C_GROUPS, PACK, Q], BF16)
+
+        banks_used = []
+
+        def next_bank():
+            tag = "bank%d" % (len(banks_used) % WORK_BANKS)
+            banks_used.append(tag)
+            return psum.tile([P, GROUP], F32, name=tag, tag=tag)
+
+        x_view = x_words.rearrange("g p n t -> p g (n t)").bitcast(I32)
+
+        def load_w(cg, kg):
+            rows = w[kg * GROUP : (kg + 1) * GROUP, cg * GROUP : (cg + 1) * GROUP]
+            nc.sync.dma_start(out=w_raw[:, cg, kg], in_=rows.rearrange("(p j) c -> p j c", j=PACK))
+
+        def load_x(kgs, tt):
+            cols = slice(tt * TOK_TILE, (tt + 1) * TOK_TILE)
+            nc.sync.dma_start(out=x_codes[:, kgs, cols].bitcast(I32), in_=x_view[:, kgs, cols])
+
+        def group_w(copy, cg, kg, ts):
+            src = w_raw[:, cg, kg].rearrange("p j (m t) -> p t m j", t=PACK)
+            copy(out=w_grouped[:, cg, kg, ts], in_=src[:, ts])
+
+        def quantize_w(cg, kg, ts):
+            cols = slice(ts.start * P, ts.stop * P)
+            nc.vector.quantize_mx(
+                out=w_codes[:, cg, kg, cols].bitcast(FP8X4),
+                scales=w_plane[:, cg, kg, cols],
+                in_=w_grouped[:, cg, kg, ts].rearrange("p t m j -> p (t m j)"),
+            )
+
+        def mx_pass(bank, u, t, kg):
+            cg, start, width = units[u]
+            w_cols = slice(t * P, (t + 1) * P)
+            x_cols = slice(start, start + width)
+            nc.tensor.matmul_mx(
+                out=bank[:, :width],
+                lhsT=w_codes[:, cg, kg, w_cols].bitcast(FP8X4),
+                lhsT_scale=w_plane[:, cg, kg, w_cols],
+                rhs=x_codes[:, kg, x_cols].bitcast(FP8X4),
+                rhs_scale=x_plane[PACK * kg :, x_cols],
+                start=(kg == 0),
+                stop=(kg == K_GROUPS - 1),
+            )
+
+        y_t = {}
+        y_grouped = {}
+
+        def epilogue(bank, u, t):
+            cg, start, width = units[u]
+            if t == 0:
+                y_t[u] = work.tile([P, PACK, width], F32, name="y_t", tag="y_t", bufs=4)
+            part = y_t[u][:, t, :]
+            nc.scalar.activation(out=part, in_=bank[:, :width], func=ACT.Relu, bias=bias_col[:, cg, t : t + 1])
+            by_image = part.rearrange("p (a q) -> p a q", q=Q)
+            nc.vector.scalar_tensor_tensor(
+                out=by_image,
+                in0=by_image,
+                scalar=gain_col[:, cg, t : t + 1],
+                in1=embed_t[:, cg, t : t + 1, :].to_broadcast([P, width // Q, Q]),
+                op0=ALU.mult,
+                op1=ALU.add,
+            )
+
+        def multiply(u, ts):
+            for t in ts:
+                bank = next_bank()
+                for kg in range(K_GROUPS):
+                    mx_pass(bank, u, t, kg)
+                epilogue(bank, u, t)
+
+        def turn(u, copies):
+            cg, start, width = units[u]
+            banks = []
+            for a in range(width // Q):
+                bank = next_bank()
+                banks.append(bank)
+                for t in range(PACK):
+                    nc.tensor.transpose(bank[:, t * P : (t + 1) * P], y_t[u][:, t, a * Q : (a + 1) * Q], ident_f32[:])
+            for a in range(width // Q):
+                y_rows = work.tile([P, P, PACK], F32, name="y_rows", tag="y_rows", bufs=8)
+                copies[a](out=y_rows[:], in_=banks[a][:].rearrange("q (t p) -> q p t", t=PACK))
+                nc.sync.dma_start(
+                    out=out_0[start // Q + a, :, cg * GROUP : (cg + 1) * GROUP],
+                    in_=y_rows[:].rearrange("q p t -> q (p t)"),
+                )
+
+        def group_y(u):
+            y_grouped[u] = work.tile([P, units[u][2], PACK], BF16, name="y_grouped", tag="y_grouped", bufs=2, align_bytes=64)
+            nc.vector.tensor_copy(out=y_grouped[u][:], in_=y_t[u][:].rearrange("p t n -> p n t"))
+
+        def quantize_y(u):
+            cg, start, width = units[u]
+            cols = slice(start, start + width)
+            nc.vector.quantize_mx(
+                out=y_codes[:, cg, cols].bitcast(FP8X4),
+                scales=y_plane[:, cg, cols],
+                in_=y_grouped[u][:].rearrange("p n t -> p (n t)"),
+            )
+            words = out_1[cg].rearrange("p n t -> p (n t)").bitcast(I32)
+            nc.sync.dma_start(out=words[:, cols], in_=y_codes[:, cg, cols].bitcast(I32))
+            if start + width == TOKENS:
+                for quad in range(4):
+                    nc.sync.dma_start(
+                        out=out_2[cg, 4 * quad : 4 * quad + 4, :].bitcast(I32),
+                        in_=y_plane[32 * quad : 32 * quad + 4, cg, :].bitcast(I32),
+                    )
+
+        nc.vector.memset(x_plane[:].bitcast(I32), 0)
+        nc.vector.memset(warm_in[:], 0.0)
+        load_w(0, 0)
+        load_x(slice(0, 1), 0)
+        nc.sync.dma_start(out=embed[:], in_=query_embed)
+        for quad in range(4):
+            nc.scalar.dma_start(
+                out=x_plane[32 * quad : 32 * quad + PACK * K_GROUPS, :].bitcast(I32),
+                in_=x_scales[:, 4 * quad : 4 * quad + 4, :].bitcast(I32),
+            )
+        nc.scalar.activation(out=warm_out[:], in_=warm_in[:], func=ACT.Relu)
+        for kg in range(1, K_GROUPS):
+            load_w(0, kg)
+            load_x(slice(kg, kg + 1), 0)
+        make_identity(nc, ident_bf16[:])
+        with nc.allow_non_contiguous_dma(reason="four channels a partition"):
+            nc.gpsimd.dma_start(out=bias_raw[:], in_=bias.rearrange("(g p t) -> p g t", p=P, t=PACK))
+            nc.gpsimd.dma_start(out=gain_raw[:], in_=gain.rearrange("(g p t) -> p g t", p=P, t=PACK))
+        make_identity(nc, ident_f32[:])
+        nc.gpsimd.tensor_copy(out=bias_col[:], in_=bias_raw[:])
+        nc.gpsimd.tensor_copy(out=gain_col[:], in_=gain_raw[:])
+        load_w(1, 0)
+        load_x(slice(0, K_GROUPS), 1)
+        load_w(1, 1)
+        load_w(1, 2)
+        for tt in range(2, TOK_TILES):
+            load_x(slice(0, K_GROUPS), tt)
+
+        embed_cols = embed[:].rearrange("q (g p t) -> q g t p", p=P, t=PACK)
+
+        low, high = slice(0, 2), slice(2, 4)
+        first_banks = [next_bank() for t in range(PACK)]
+        for kg in range(K_GROUPS):
+            group_w(nc.vector.tensor_copy, 0, kg, low)
+            group_w(nc.scalar.copy, 0, kg, high)
+            quantize_w(0, kg, low)
+            quantize_w(0, kg, high)
+            for t in range(PACK):
+                mx_pass(first_banks[t], 0, t, kg)
+            if kg == 0:
+                for cg in range(C_GROUPS):
+                    for t in range(PACK):
+                        nc.tensor.transpose(embed_t[:, cg, t, :], embed_cols[:, cg, t, :], ident_bf16[:])
+        group_w(nc.vector.tensor_copy, 1, 0, low)
+        group_w(nc.scalar.copy, 1, 0, high)
+        quantize_w(1, 0, slice(0, PACK))
+        for t in range(PACK):
+            epilogue(first_banks[t], 0, t)
+
+        scalar_only = [nc.scalar.copy] * IMAGES
+        for u in range(1, len(units)):
+            multiply(u, range(1))
+            if u > 1:
+                quantize_y(u - 2)
+            multiply(u, range(1, BEFORE_TURN))
+            turn(u - 1, scalar_only)
+            if u < K_GROUPS:
+                group_w(nc.vector.tensor_copy, 1, u, slice(0, PACK))
+            group_y(u - 1)
+            if u < K_GROUPS:
+                quantize_w(1, u, slice(0, PACK))
+            multiply(u, range(BEFORE_TURN, PACK))
+        quantize_y(last - 1)
+        group_y(last)
+        turn(last, scalar_only)
+        quantize_y(last)

@@ -25,8 +25,14 @@ TOK_TILE = 512
 TOK_TILES = TOKENS // TOK_TILE
 IMAGES = TOK_TILE // Q
 WORK_BANKS = 7
-UNIT_WIDTHS = ((512, 512, 512, 512), (512, 512, 512, 256, 256))
-BEFORE_TURN = 3
+UNIT_WIDTHS = ((512, 512, 512, 512), (512, 512, 512, 512))
+BEFORE_TURN = (4, 4, 4, 4, 4, 4, 4, 2)
+ROWS_ON_VECTOR = (0, 0, 0, 0, 0, 0, 0, 1, 1)
+ON_GPSIMD = (0, 3, 3, 3, 3, 3, 3, 3)
+ON_VECTOR = (0, 0, 1, 2, 2, 1, 1, 0)
+Y_T_BUFS = 6
+HEAD_GROUPS = 4
+ROWS_FIRST = 1
 
 
 def tile_mask_query_embed_planes_g6_kernel(tc, x_words, x_scales, w, bias, gain, query_embed, out_0, out_1, out_2):
@@ -48,7 +54,6 @@ def tile_mask_query_embed_planes_g6_kernel(tc, x_words, x_scales, w, bias, gain,
         x_codes = keep.tile([P, K_GROUPS, TOKENS], U32, align_bytes=64)
         x_plane = keep.tile([P, TOKENS], U8, align_bytes=64)
         w_raw = keep.tile([P, C_GROUPS, K_GROUPS, PACK, GROUP], BF16, align_bytes=64)
-        w_grouped = keep.tile([P, C_GROUPS, K_GROUPS, PACK, P, PACK], BF16, align_bytes=64)
         w_codes = keep.tile([P, C_GROUPS, K_GROUPS, GROUP], U32, align_bytes=64)
         w_plane = keep.tile([P, C_GROUPS, K_GROUPS, GROUP], U8, align_bytes=64)
         y_codes = keep.tile([P, C_GROUPS, TOKENS], U32, align_bytes=64)
@@ -77,20 +82,30 @@ def tile_mask_query_embed_planes_g6_kernel(tc, x_words, x_scales, w, bias, gain,
             rows = w[kg * GROUP : (kg + 1) * GROUP, cg * GROUP : (cg + 1) * GROUP]
             nc.sync.dma_start(out=w_raw[:, cg, kg], in_=rows.rearrange("(p j) c -> p j c", j=PACK))
 
-        def load_x(kgs, tt):
-            cols = slice(tt * TOK_TILE, (tt + 1) * TOK_TILE)
+        def load_x(kgs, t0, t1):
+            cols = slice(t0 * TOK_TILE, t1 * TOK_TILE)
             nc.sync.dma_start(out=x_codes[:, kgs, cols].bitcast(I32), in_=x_view[:, kgs, cols])
 
-        def group_w(copy, cg, kg, ts):
-            src = w_raw[:, cg, kg].rearrange("p j (m t) -> p t m j", t=PACK)
-            copy(out=w_grouped[:, cg, kg, ts], in_=src[:, ts])
+        def load_scales(queue, cols):
+            for quad in range(4):
+                queue.dma_start(
+                    out=x_plane[32 * quad : 32 * quad + PACK * K_GROUPS, cols].bitcast(I32),
+                    in_=x_scales[:, 4 * quad : 4 * quad + 4, cols].bitcast(I32),
+                )
 
-        def quantize_w(cg, kg, ts):
+        def stage(tag, bufs=1):
+            return work.tile([P, PACK, P, PACK], BF16, name=tag, tag=tag, bufs=bufs, align_bytes=64)
+
+        def group_w(copy, staged, cg, kg, ts):
+            src = w_raw[:, cg, kg].rearrange("p j (m t) -> p t m j", t=PACK)
+            copy(out=staged[:, ts], in_=src[:, ts])
+
+        def quantize_w(staged, cg, kg, ts):
             cols = slice(ts.start * P, ts.stop * P)
             nc.vector.quantize_mx(
                 out=w_codes[:, cg, kg, cols].bitcast(FP8X4),
                 scales=w_plane[:, cg, kg, cols],
-                in_=w_grouped[:, cg, kg, ts].rearrange("p t m j -> p (t m j)"),
+                in_=staged[:, ts].rearrange("p t m j -> p (t m j)"),
             )
 
         def mx_pass(bank, u, t, kg):
@@ -109,14 +124,18 @@ def tile_mask_query_embed_planes_g6_kernel(tc, x_words, x_scales, w, bias, gain,
 
         y_t = {}
         y_grouped = {}
+        z_bank = {}
+        row_bank = {}
 
-        def epilogue(bank, u, t):
+        def relu(u, t):
             cg, start, width = units[u]
             if t == 0:
-                y_t[u] = work.tile([P, PACK, width], F32, name="y_t", tag="y_t", bufs=4)
-            part = y_t[u][:, t, :]
-            nc.scalar.activation(out=part, in_=bank[:, :width], func=ACT.Relu, bias=bias_col[:, cg, t : t + 1])
-            by_image = part.rearrange("p (a q) -> p a q", q=Q)
+                y_t[u] = work.tile([P, PACK, width], F32, name="y_t", tag="y_t", bufs=Y_T_BUFS)
+            nc.scalar.activation(out=y_t[u][:, t, :], in_=z_bank[u, t][:, :width], func=ACT.Relu, bias=bias_col[:, cg, t : t + 1])
+
+        def finish(u, t):
+            cg, start, width = units[u]
+            by_image = y_t[u][:, t, :].rearrange("p (a q) -> p a q", q=Q)
             nc.vector.scalar_tensor_tensor(
                 out=by_image,
                 in0=by_image,
@@ -128,39 +147,81 @@ def tile_mask_query_embed_planes_g6_kernel(tc, x_words, x_scales, w, bias, gain,
 
         def multiply(u, ts):
             for t in ts:
-                bank = next_bank()
-                for kg in range(K_GROUPS):
-                    mx_pass(bank, u, t, kg)
-                epilogue(bank, u, t)
+                if (u, t) not in z_bank:
+                    z_bank[u, t] = next_bank()
+                    for kg in range(K_GROUPS):
+                        mx_pass(z_bank[u, t], u, t, kg)
+                relu(u, t)
+                finish(u, t)
 
-        def turn(u, copies):
+        def turn(u):
+            images = range(units[u][2] // Q)
+            for a in images:
+                row_bank[u, a] = next_bank()
+            order = [(a, t) for a in images for t in range(PACK)]
+            if u == last:
+                order = [(a, t) for t in range(PACK) for a in images]
+            for a, t in order:
+                nc.tensor.transpose(row_bank[u, a][:, t * P : (t + 1) * P], y_t[u][:, t, a * Q : (a + 1) * Q], ident_f32[:])
+
+        def store_rows(u, on_vector):
             cg, start, width = units[u]
-            banks = []
-            for a in range(width // Q):
-                bank = next_bank()
-                banks.append(bank)
-                for t in range(PACK):
-                    nc.tensor.transpose(bank[:, t * P : (t + 1) * P], y_t[u][:, t, a * Q : (a + 1) * Q], ident_f32[:])
-            for a in range(width // Q):
-                y_rows = work.tile([P, P, PACK], F32, name="y_rows", tag="y_rows", bufs=8)
-                copies[a](out=y_rows[:], in_=banks[a][:].rearrange("q (t p) -> q p t", t=PACK))
+            images = width // Q
+            for a in range(images):
+                copy = nc.vector.tensor_copy if a >= images - on_vector else nc.scalar.copy
+                y_rows = work.tile([P, P, PACK], F32, name="y_rows", tag="y_rows", bufs=12)
+                copy(out=y_rows[:], in_=row_bank[u, a][:].rearrange("q (t p) -> q p t", t=PACK))
                 nc.sync.dma_start(
                     out=out_0[start // Q + a, :, cg * GROUP : (cg + 1) * GROUP],
                     in_=y_rows[:].rearrange("q p t -> q (p t)"),
                 )
 
-        def group_y(u):
-            y_grouped[u] = work.tile([P, units[u][2], PACK], BF16, name="y_grouped", tag="y_grouped", bufs=2, align_bytes=64)
-            nc.vector.tensor_copy(out=y_grouped[u][:], in_=y_t[u][:].rearrange("p t n -> p n t"))
+        images_left = [(u, a) for u in range(len(units)) for a in range(units[u][2] // Q)]
+        quantized = []
+        planes_stored = []
 
-        def quantize_y(u):
+        def group_y(count, tag, on_gpsimd):
+            taken = images_left[:count]
+            for image in taken:
+                images_left.remove(image)
+            staged = stage(tag)
+            pieces = []
+            slot = 0
+            for u in sorted(set(u for u, a in taken)):
+                mine = [a for v, a in taken if v == u]
+                src = y_t[u][:, :, mine[0] * Q : (mine[-1] + 1) * Q].rearrange("p t n -> p n t")
+                dst = staged[:, slot : slot + len(mine)].rearrange("p a q t -> p (a q) t")
+                if on_gpsimd:
+                    nc.gpsimd.tensor_scalar(out=dst, in0=src, scalar1=1.0, scalar2=-0.0, op0=ALU.mult, op1=ALU.add)
+                else:
+                    nc.vector.tensor_copy(out=dst, in_=src)
+                sizes = {1: (1,), 2: (1, 1) if on_gpsimd else (2,), 3: (2, 1), 4: (2, 2) if on_gpsimd else (4,)}[len(mine)]
+                first_image = mine[0]
+                for size in sizes:
+                    pieces.append((staged, slot, u, first_image, size))
+                    slot += size
+                    first_image += size
+            return pieces
+
+        def quantize_y(staged, slot, u, first_image, size):
             cg, start, width = units[u]
-            cols = slice(start, start + width)
+            cols = slice(start + first_image * Q, start + (first_image + size) * Q)
             nc.vector.quantize_mx(
                 out=y_codes[:, cg, cols].bitcast(FP8X4),
                 scales=y_plane[:, cg, cols],
-                in_=y_grouped[u][:].rearrange("p n t -> p (n t)"),
+                in_=staged[:, slot : slot + size].rearrange("p a q t -> p (a q t)"),
             )
+            quantized.extend((u, first_image + a) for a in range(size))
+
+        def store_ready_planes():
+            for u in range(len(units)):
+                if u not in planes_stored and all((u, a) in quantized for a in range(units[u][2] // Q)):
+                    planes_stored.append(u)
+                    store_planes(u)
+
+        def store_planes(u):
+            cg, start, width = units[u]
+            cols = slice(start, start + width)
             words = out_1[cg].rearrange("p n t -> p (n t)").bitcast(I32)
             nc.sync.dma_start(out=words[:, cols], in_=y_codes[:, cg, cols].bitcast(I32))
             if start + width == TOKENS:
@@ -170,20 +231,34 @@ def tile_mask_query_embed_planes_g6_kernel(tc, x_words, x_scales, w, bias, gain,
                         in_=y_plane[32 * quad : 32 * quad + 4, cg, :].bitcast(I32),
                     )
 
+        def prepare_w(tag, kg):
+            staged = stage(tag)
+            halves = (slice(0, 2), slice(2, 4))
+            for half in halves:
+                group_w(nc.vector.tensor_copy, staged, 1, kg, half)
+            for half in halves:
+                quantize_w(staged, 1, kg, half)
+
+        def port_work(u, from_gpsimd):
+            if from_gpsimd:
+                quantize_y(*from_gpsimd[-1])
+            if u + 1 < K_GROUPS:
+                prepare_w("stage_b" if from_gpsimd else "stage_a", u + 1)
+            mine = group_y(ON_VECTOR[u], "stage_b", False) if ON_VECTOR[u] else []
+            middle = from_gpsimd[1:-1]
+            for piece in middle + mine + from_gpsimd[:1 if len(from_gpsimd) > 1 else 0]:
+                quantize_y(*piece)
+
         nc.vector.memset(x_plane[:].bitcast(I32), 0)
         nc.vector.memset(warm_in[:], 0.0)
         load_w(0, 0)
-        load_x(slice(0, 1), 0)
-        nc.sync.dma_start(out=embed[:], in_=query_embed)
-        for quad in range(4):
-            nc.scalar.dma_start(
-                out=x_plane[32 * quad : 32 * quad + PACK * K_GROUPS, :].bitcast(I32),
-                in_=x_scales[:, 4 * quad : 4 * quad + 4, :].bitcast(I32),
-            )
+        load_x(slice(0, 1), 0, 1)
+        load_scales(nc.scalar, slice(0, TOK_TILE))
         nc.scalar.activation(out=warm_out[:], in_=warm_in[:], func=ACT.Relu)
-        for kg in range(1, K_GROUPS):
-            load_w(0, kg)
-            load_x(slice(kg, kg + 1), 0)
+        load_w(0, 1)
+        load_w(0, 2)
+        load_x(slice(1, K_GROUPS), 0, 1)
+        nc.sync.dma_start(out=embed[:], in_=query_embed)
         make_identity(nc, ident_bf16[:])
         with nc.allow_non_contiguous_dma(reason="four channels a partition"):
             nc.gpsimd.dma_start(out=bias_raw[:], in_=bias.rearrange("(g p t) -> p g t", p=P, t=PACK))
@@ -192,47 +267,54 @@ def tile_mask_query_embed_planes_g6_kernel(tc, x_words, x_scales, w, bias, gain,
         nc.gpsimd.tensor_copy(out=bias_col[:], in_=bias_raw[:])
         nc.gpsimd.tensor_copy(out=gain_col[:], in_=gain_raw[:])
         load_w(1, 0)
-        load_x(slice(0, K_GROUPS), 1)
+        load_scales(nc.sync, slice(TOK_TILE, TOKENS))
+        for kg in range(K_GROUPS):
+            load_x(slice(kg, kg + 1), 1, 2)
         load_w(1, 1)
+        load_x(slice(0, K_GROUPS), 2, 3)
         load_w(1, 2)
-        for tt in range(2, TOK_TILES):
-            load_x(slice(0, K_GROUPS), tt)
+        load_x(slice(0, K_GROUPS), 3, 4)
 
         embed_cols = embed[:].rearrange("q (g p t) -> q g t p", p=P, t=PACK)
-
-        low, high = slice(0, 2), slice(2, 4)
-        first_banks = [next_bank() for t in range(PACK)]
+        first = [divmod(i, PACK) for i in range(HEAD_GROUPS)]
+        for ut in first:
+            z_bank[ut] = next_bank()
         for kg in range(K_GROUPS):
-            group_w(nc.vector.tensor_copy, 0, kg, low)
-            group_w(nc.scalar.copy, 0, kg, high)
-            quantize_w(0, kg, low)
-            quantize_w(0, kg, high)
-            for t in range(PACK):
-                mx_pass(first_banks[t], 0, t, kg)
-            if kg == 0:
+            staged = stage("stage_head", bufs=K_GROUPS)
+            group_w(nc.vector.tensor_copy, staged, 0, kg, slice(0, 1))
+            group_w(nc.scalar.copy, staged, 0, kg, slice(3, 4))
+            group_w(nc.vector.tensor_copy, staged, 0, kg, slice(1, 2))
+            quantize_w(staged, 0, kg, slice(0, 1))
+            group_w(nc.vector.tensor_copy, staged, 0, kg, slice(2, 3))
+            quantize_w(staged, 0, kg, slice(1, 2))
+            quantize_w(staged, 0, kg, slice(2, 4))
+            for u, t in first:
+                mx_pass(z_bank[u, t], u, t, kg)
+            if kg == K_GROUPS - 1:
                 for cg in range(C_GROUPS):
                     for t in range(PACK):
                         nc.tensor.transpose(embed_t[:, cg, t, :], embed_cols[:, cg, t, :], ident_bf16[:])
-        group_w(nc.vector.tensor_copy, 1, 0, low)
-        group_w(nc.scalar.copy, 1, 0, high)
-        quantize_w(1, 0, slice(0, PACK))
-        for t in range(PACK):
-            epilogue(first_banks[t], 0, t)
+        prepare_w("stage_b", 0)
+        multiply(0, range(PACK))
+        port_work(0, [])
 
-        scalar_only = [nc.scalar.copy] * IMAGES
         for u in range(1, len(units)):
-            multiply(u, range(1))
-            if u > 1:
-                quantize_y(u - 2)
-            multiply(u, range(1, BEFORE_TURN))
-            turn(u - 1, scalar_only)
-            if u < K_GROUPS:
-                group_w(nc.vector.tensor_copy, 1, u, slice(0, PACK))
-            group_y(u - 1)
-            if u < K_GROUPS:
-                quantize_w(1, u, slice(0, PACK))
-            multiply(u, range(BEFORE_TURN, PACK))
-        quantize_y(last - 1)
-        group_y(last)
-        turn(last, scalar_only)
-        quantize_y(last)
+            before = BEFORE_TURN[u]
+            from_gpsimd = group_y(ON_GPSIMD[u], "stage_a", True) if ON_GPSIMD[u] else []
+            multiply(u, range(before))
+            turn(u - 1)
+            if ROWS_FIRST:
+                store_rows(u - 1, ROWS_ON_VECTOR[u])
+            multiply(u, range(before, PACK))
+            if not ROWS_FIRST:
+                store_rows(u - 1, ROWS_ON_VECTOR[u])
+            store_ready_planes()
+            port_work(u, from_gpsimd)
+        turn(last)
+        store_ready_planes()
+        assert len(images_left) <= PACK
+        mine = group_y(len(images_left), "stage_b", False)
+        store_rows(last, ROWS_ON_VECTOR[last + 1])
+        for piece in mine:
+            quantize_y(*piece)
+        store_ready_planes()

from contextlib import ExitStack

import concourse.mybir as mybir
from concourse.masks import make_identity

B, Q, D, C = 16, 128, 1536, 1024
TOKENS = B * Q
FLOPS = 2 * TOKENS * D * C

F32 = mybir.dt.float32
BF16 = mybir.dt.bfloat16
I32 = mybir.dt.int32
U32 = mybir.dt.uint32
U8 = mybir.dt.uint8
FP8X4 = mybir.dt.float8_e4m3fn_x4
ALU = mybir.AluOpType
ACT = mybir.ActivationFunctionType

P = 128
PACK = 4
GROUP = P * PACK
K_GROUPS = D // GROUP
C_GROUPS = C // GROUP
TOK_TILE = 512
TOK_TILES = TOKENS // TOK_TILE
IMAGES = TOK_TILE // Q
WORK_BANKS = 7
UNIT_WIDTHS = ((512, 512, 512, 512), (512, 512, 512, 512))
BEFORE_TURN = (4, 4, 4, 4, 4, 4, 4, 2)
ROWS_ON_VECTOR = (0, 0, 0, 0, 0, 0, 0, 1, 1)
ON_GPSIMD = (0, 3, 3, 3, 3, 3, 3, 3)
ON_VECTOR = (0, 0, 1, 2, 2, 1, 1, 0)
Y_T_BUFS = 6
HEAD_GROUPS = 4
ROWS_FIRST = 1


def tile_mask_query_embed_planes_g6_kernel(tc, x_words, x_scales, w, bias, gain, query_embed, out_0, out_1, out_2):
    nc = tc.nc
    units = []
    for cg, widths in enumerate(UNIT_WIDTHS):
        start = 0
        for width in widths:
            units.append((cg, start, width))
            start += width
    last = len(units) - 1

    with ExitStack() as ctx:
        keep = ctx.enter_context(tc.tile_pool(name="keep", bufs=1))
        work = ctx.enter_context(tc.tile_pool(name="work", bufs=2))
        psum = ctx.enter_context(tc.psum_pool(name="psum", bufs=1))
        ctx.enter_context(tc.manual_schedule())

        x_codes = keep.tile([P, K_GROUPS, TOKENS], U32, align_bytes=64)
        x_plane = keep.tile([P, TOKENS], U8, align_bytes=64)
        w_raw = keep.tile([P, C_GROUPS, K_GROUPS, PACK, GROUP], BF16, align_bytes=64)
        w_codes = keep.tile([P, C_GROUPS, K_GROUPS, GROUP], U32, align_bytes=64)
        w_plane = keep.tile([P, C_GROUPS, K_GROUPS, GROUP], U8, align_bytes=64)
        y_codes = keep.tile([P, C_GROUPS, TOKENS], U32, align_bytes=64)
        y_plane = keep.tile([P, C_GROUPS, TOKENS], U8, align_bytes=64)
        embed = keep.tile([P, C], BF16)
        bias_raw = keep.tile([P, C_GROUPS, PACK], BF16)
        gain_raw = keep.tile([P, C_GROUPS, PACK], BF16)
        bias_col = keep.tile([P, C_GROUPS, PACK], F32)
        gain_col = keep.tile([P, C_GROUPS, PACK], F32)
        ident_bf16 = keep.tile([P, P], BF16)
        ident_f32 = keep.tile([P, P], F32)
        warm_in = keep.tile([P, 1], F32)
        warm_out = keep.tile([P, 1], F32)
        embed_t = psum.tile([P, C_GROUPS, PACK, Q], BF16)

        banks_used = []

        def next_bank():
            tag = "bank%d" % (len(banks_used) % WORK_BANKS)
            banks_used.append(tag)
            return psum.tile([P, GROUP], F32, name=tag, tag=tag)

        x_view = x_words.rearrange("g p n t -> p g (n t)").bitcast(I32)

        def load_w(cg, kg):
            rows = w[kg * GROUP : (kg + 1) * GROUP, cg * GROUP : (cg + 1) * GROUP]
            nc.sync.dma_start(out=w_raw[:, cg, kg], in_=rows.rearrange("(p j) c -> p j c", j=PACK))

        def load_x(kgs, t0, t1):
            cols = slice(t0 * TOK_TILE, t1 * TOK_TILE)
            nc.sync.dma_start(out=x_codes[:, kgs, cols].bitcast(I32), in_=x_view[:, kgs, cols])

        def load_scales(queue, cols):
            for quad in range(4):
                queue.dma_start(
                    out=x_plane[32 * quad : 32 * quad + PACK * K_GROUPS, cols].bitcast(I32),
                    in_=x_scales[:, 4 * quad : 4 * quad + 4, cols].bitcast(I32),
                )

        def stage(tag, bufs=1):
            return work.tile([P, PACK, P, PACK], BF16, name=tag, tag=tag, bufs=bufs, align_bytes=64)

        def group_w(copy, staged, cg, kg, ts):
            src = w_raw[:, cg, kg].rearrange("p j (m t) -> p t m j", t=PACK)
            copy(out=staged[:, ts], in_=src[:, ts])

        def quantize_w(staged, cg, kg, ts):
            cols = slice(ts.start * P, ts.stop * P)
            nc.vector.quantize_mx(
                out=w_codes[:, cg, kg, cols].bitcast(FP8X4),
                scales=w_plane[:, cg, kg, cols],
                in_=staged[:, ts].rearrange("p t m j -> p (t m j)"),
            )

        def mx_pass(bank, u, t, kg):
            cg, start, width = units[u]
            w_cols = slice(t * P, (t + 1) * P)
            x_cols = slice(start, start + width)
            nc.tensor.matmul_mx(
                out=bank[:, :width],
                lhsT=w_codes[:, cg, kg, w_cols].bitcast(FP8X4),
                lhsT_scale=w_plane[:, cg, kg, w_cols],
                rhs=x_codes[:, kg, x_cols].bitcast(FP8X4),
                rhs_scale=x_plane[PACK * kg :, x_cols],
                start=(kg == 0),
                stop=(kg == K_GROUPS - 1),
            )

        y_t = {}
        y_grouped = {}
        z_bank = {}
        row_bank = {}

        def relu(u, t):
            cg, start, width = units[u]
            if t == 0:
                y_t[u] = work.tile([P, PACK, width], F32, name="y_t", tag="y_t", bufs=Y_T_BUFS)
            nc.scalar.activation(out=y_t[u][:, t, :], in_=z_bank[u, t][:, :width], func=ACT.Relu, bias=bias_col[:, cg, t : t + 1])

        def finish(u, t):
            cg, start, width = units[u]
            by_image = y_t[u][:, t, :].rearrange("p (a q) -> p a q", q=Q)
            nc.vector.scalar_tensor_tensor(
                out=by_image,
                in0=by_image,
                scalar=gain_col[:, cg, t : t + 1],
                in1=embed_t[:, cg, t : t + 1, :].to_broadcast([P, width // Q, Q]),
                op0=ALU.mult,
                op1=ALU.add,
            )

        def multiply(u, ts):
            for t in ts:
                if (u, t) not in z_bank:
                    z_bank[u, t] = next_bank()
                    for kg in range(K_GROUPS):
                        mx_pass(z_bank[u, t], u, t, kg)
                relu(u, t)
                finish(u, t)

        def turn(u):
            images = range(units[u][2] // Q)
            for a in images:
                row_bank[u, a] = next_bank()
            order = [(a, t) for a in images for t in range(PACK)]
            if u == last:
                order = [(a, t) for t in range(PACK) for a in images]
            for a, t in order:
                nc.tensor.transpose(row_bank[u, a][:, t * P : (t + 1) * P], y_t[u][:, t, a * Q : (a + 1) * Q], ident_f32[:])

        def store_rows(u, on_vector):
            cg, start, width = units[u]
            images = width // Q
            for a in range(images):
                copy = nc.vector.tensor_copy if a >= images - on_vector else nc.scalar.copy
                y_rows = work.tile([P, P, PACK], F32, name="y_rows", tag="y_rows", bufs=12)
                copy(out=y_rows[:], in_=row_bank[u, a][:].rearrange("q (t p) -> q p t", t=PACK))
                nc.sync.dma_start(
                    out=out_0[start // Q + a, :, cg * GROUP : (cg + 1) * GROUP],
                    in_=y_rows[:].rearrange("q p t -> q (p t)"),
                )

        images_left = [(u, a) for u in range(len(units)) for a in range(units[u][2] // Q)]
        quantized = []
        planes_stored = []

        def group_y(count, tag, on_gpsimd):
            taken = images_left[:count]
            for image in taken:
                images_left.remove(image)
            staged = stage(tag)
            pieces = []
            slot = 0
            for u in sorted(set(u for u, a in taken)):
                mine = [a for v, a in taken if v == u]
                src = y_t[u][:, :, mine[0] * Q : (mine[-1] + 1) * Q].rearrange("p t n -> p n t")
                dst = staged[:, slot : slot + len(mine)].rearrange("p a q t -> p (a q) t")
                if on_gpsimd:
                    nc.gpsimd.tensor_scalar(out=dst, in0=src, scalar1=1.0, scalar2=-0.0, op0=ALU.mult, op1=ALU.add)
                else:
                    nc.vector.tensor_copy(out=dst, in_=src)
                sizes = {1: (1,), 2: (1, 1) if on_gpsimd else (2,), 3: (2, 1), 4: (2, 2) if on_gpsimd else (4,)}[len(mine)]
                first_image = mine[0]
                for size in sizes:
                    pieces.append((staged, slot, u, first_image, size))
                    slot += size
                    first_image += size
            return pieces

        def quantize_y(staged, slot, u, first_image, size):
            cg, start, width = units[u]
            cols = slice(start + first_image * Q, start + (first_image + size) * Q)
            nc.vector.quantize_mx(
                out=y_codes[:, cg, cols].bitcast(FP8X4),
                scales=y_plane[:, cg, cols],
                in_=staged[:, slot : slot + size].rearrange("p a q t -> p (a q t)"),
            )
            quantized.extend((u, first_image + a) for a in range(size))

        def store_ready_planes():
            for u in range(len(units)):
                if u not in planes_stored and all((u, a) in quantized for a in range(units[u][2] // Q)):
                    planes_stored.append(u)
                    store_planes(u)

        def store_planes(u):
            cg, start, width = units[u]
            cols = slice(start, start + width)
            words = out_1[cg].rearrange("p n t -> p (n t)").bitcast(I32)
            nc.sync.dma_start(out=words[:, cols], in_=y_codes[:, cg, cols].bitcast(I32))
            if start + width == TOKENS:
                for quad in range(4):
                    nc.sync.dma_start(
                        out=out_2[cg, 4 * quad : 4 * quad + 4, :].bitcast(I32),
                        in_=y_plane[32 * quad : 32 * quad + 4, cg, :].bitcast(I32),
                    )

        def prepare_w(tag, kg):
            staged = stage(tag)
            halves = (slice(0, 2), slice(2, 4))
            for half in halves:
                group_w(nc.vector.tensor_copy, staged, 1, kg, half)
            for half in halves:
                quantize_w(staged, 1, kg, half)

        def port_work(u, from_gpsimd):
            if from_gpsimd:
                quantize_y(*from_gpsimd[-1])
            if u + 1 < K_GROUPS:
                prepare_w("stage_b" if from_gpsimd else "stage_a", u + 1)
            mine = group_y(ON_VECTOR[u], "stage_b", False) if ON_VECTOR[u] else []
            middle = from_gpsimd[1:-1]
            for piece in middle + mine + from_gpsimd[:1 if len(from_gpsimd) > 1 else 0]:
                quantize_y(*piece)

        nc.vector.memset(x_plane[:].bitcast(I32), 0)
        nc.vector.memset(warm_in[:], 0.0)
        load_w(0, 0)
        load_x(slice(0, 1), 0, 1)
        load_scales(nc.scalar, slice(0, TOK_TILE))
        nc.scalar.activation(out=warm_out[:], in_=warm_in[:], func=ACT.Relu)
        load_w(0, 1)
        load_w(0, 2)
        load_x(slice(1, K_GROUPS), 0, 1)
        nc.sync.dma_start(out=embed[:], in_=query_embed)
        make_identity(nc, ident_bf16[:])
        with nc.allow_non_contiguous_dma(reason="four channels a partition"):
            nc.gpsimd.dma_start(out=bias_raw[:], in_=bias.rearrange("(g p t) -> p g t", p=P, t=PACK))
            nc.gpsimd.dma_start(out=gain_raw[:], in_=gain.rearrange("(g p t) -> p g t", p=P, t=PACK))
        make_identity(nc, ident_f32[:])
        nc.gpsimd.tensor_copy(out=bias_col[:], in_=bias_raw[:])
        nc.gpsimd.tensor_copy(out=gain_col[:], in_=gain_raw[:])
        load_w(1, 0)
        load_scales(nc.sync, slice(TOK_TILE, TOKENS))
        for kg in range(K_GROUPS):
            load_x(slice(kg, kg + 1), 1, 2)
        load_w(1, 1)
        load_x(slice(0, K_GROUPS), 2, 3)
        load_w(1, 2)
        load_x(slice(0, K_GROUPS), 3, 4)

        embed_cols = embed[:].rearrange("q (g p t) -> q g t p", p=P, t=PACK)
        first = [divmod(i, PACK) for i in range(HEAD_GROUPS)]
        for ut in first:
            z_bank[ut] = next_bank()
        for kg in range(K_GROUPS):
            staged = stage("stage_head", bufs=K_GROUPS)
            group_w(nc.vector.tensor_copy, staged, 0, kg, slice(0, 1))
            group_w(nc.scalar.copy, staged, 0, kg, slice(3, 4))
            group_w(nc.vector.tensor_copy, staged, 0, kg, slice(1, 2))
            quantize_w(staged, 0, kg, slice(0, 1))
            group_w(nc.vector.tensor_copy, staged, 0, kg, slice(2, 3))
            quantize_w(staged, 0, kg, slice(1, 2))
            quantize_w(staged, 0, kg, slice(2, 4))
            for u, t in first:
                mx_pass(z_bank[u, t], u, t, kg)
            if kg == K_GROUPS - 1:
                for cg in range(C_GROUPS):
                    for t in range(PACK):
                        nc.tensor.transpose(embed_t[:, cg, t, :], embed_cols[:, cg, t, :], ident_bf16[:])
        prepare_w("stage_b", 0)
        multiply(0, range(PACK))
        port_work(0, [])

        for u in range(1, len(units)):
            before = BEFORE_TURN[u]
            from_gpsimd = group_y(ON_GPSIMD[u], "stage_a", True) if ON_GPSIMD[u] else []
            multiply(u, range(before))
            turn(u - 1)
            if ROWS_FIRST:
                store_rows(u - 1, ROWS_ON_VECTOR[u])
            multiply(u, range(before, PACK))
            if not ROWS_FIRST:
                store_rows(u - 1, ROWS_ON_VECTOR[u])
            store_ready_planes()
            port_work(u, from_gpsimd)
        turn(last)
        store_ready_planes()
        assert len(images_left) <= PACK
        mine = group_y(len(images_left), "stage_b", False)
        store_rows(last, ROWS_ON_VECTOR[last + 1])
        for piece in mine:
            quantize_y(*piece)
        store_ready_planes()
